import numpy as np
import ml_dtypes


def mxq(x, axis, fmt="e4m3"):
    dtype, down = {"e4m3": (ml_dtypes.float8_e4m3fn, 7), "e5m2": (ml_dtypes.float8_e5m2, 14)}[fmt]
    v = np.moveaxis(np.asarray(x, np.float32).astype(ml_dtypes.bfloat16).astype(np.float64), axis, -1)
    blocks = v.reshape(v.shape[:-1] + (-1, 32))
    amax = np.abs(blocks).max(-1, keepdims=True)
    byte = np.maximum(np.where(amax > 0, np.frexp(amax)[1] - 1 + 127, 0) - down, 1)
    scale = np.exp2(byte - 127.0)
    codes = (blocks / scale).astype(np.float32).astype(dtype).astype(np.float64)
    return np.moveaxis((codes * scale).reshape(v.shape), -1, axis)


WIDE = False


def mx_kscale(k):
    if not WIDE:
        return np.ones(k)
    levels = np.array([10, -10, 5, -5, 0])
    if k % 512:
        return np.exp2(np.random.permutation(np.resize(levels, k // 32))).repeat(32)
    a = np.empty((k // 512, 16))
    for p in range(k // 512):
        a[p, :8] = np.random.permutation(np.resize(levels, 8))
        for g in range(8):
            far = levels[np.abs(levels - a[p, g]) >= 10]
            a[p, g + 8] = far[np.random.randint(len(far))]
    return np.exp2(a.ravel()).repeat(32)


def f64(x):
    return np.asarray(x).astype(np.float64)


def striped8(idx):
    return np.asarray(idx).reshape(8, -1, 16).transpose(0, 2, 1).reshape(128, -1).astype(np.uint16)


def unstriped8(offs):
    return offs.reshape(8, 16, -1).transpose(0, 2, 1).reshape(8, -1).astype(np.int64)


def pick8(x, idx, run):
    r = np.arange(len(x))
    return x[r[:, None], idx[r % (8 * run) // run]]


E2M1 = np.array([0.0, 0.5, 1.0, 1.5, 2.0, 3.0, 4.0, 6.0, -0.0, -0.5, -1.0, -1.5, -2.0, -3.0, -4.0, -6.0])


def pack_weight(w, fmt):
    k, n = w.shape
    w = f64(np.asarray(w, np.float32).astype(ml_dtypes.bfloat16)).reshape(k // 32, 32, n)
    amax = np.abs(w).max(1)
    if fmt == "e4m3":
        byte = np.frexp(amax)[1] - 1 + 127 - 7
    else:
        mant, ex = np.frexp(amax / 6.0)
        byte = np.where(mant > 0.5, ex, ex - 1) + 127
    byte = np.clip(np.where(amax > 0, byte, 1), 1, 254)
    scaled = (w * np.exp2(127.0 - byte)[:, None, :]).reshape(k, n).astype(np.float32)
    by_word = np.ascontiguousarray(scaled.reshape(k // 512, 128, 4, n).transpose(0, 1, 3, 2))
    if fmt == "e4m3":
        words = by_word.astype(ml_dtypes.float8_e4m3fn).view(np.uint8)
    else:
        c = by_word.astype(ml_dtypes.float4_e2m1fn).view(np.uint8) & 0xF
        words = (c[..., 0::2] | (c[..., 1::2] << 4)).reshape(k // 512, 128, 2 * n)
    return np.ascontiguousarray(words), np.ascontiguousarray(byte.astype(np.uint8).reshape(k // 512, 16, n))


def unpack_weight(words, scales, fmt):
    g, _, n = scales.shape
    words = np.ascontiguousarray(words).reshape(g, 128, n, -1)
    if fmt == "e4m3":
        vals = words.view(ml_dtypes.float8_e4m3fn).astype(np.float64)
    else:
        nib = np.empty((g, 128, n, 4), np.uint8)
        nib[..., 0::2] = words & 0xF
        nib[..., 1::2] = words >> 4
        vals = E2M1[nib]
    vals = vals * np.repeat(np.exp2(scales.astype(np.float64) - 127.0), 8, axis=1)[..., None]
    return vals.transpose(0, 1, 3, 2).reshape(g * 512, n)


C, D, I, Z, J, Q = 512, 512, 256, 512, 256, 128


def setup_inputs():
    n = np.random.standard_normal
    idx = np.stack([np.random.permutation(Z)[:I] for _ in range(8)])
    idx2 = np.stack([np.random.permutation(Z)[:I] for _ in range(8)])
    idx3 = np.stack([np.random.permutation(Z)[:J] for _ in range(8)])
    idx4 = np.stack([np.random.permutation(Z)[:J] for _ in range(8)])
    idx5 = np.stack([np.random.permutation(Z)[:J] for _ in range(8)])
    fc = mx_kscale(C)
    fd = mx_kscale(D)
    wpp = pack_weight(n((C, D)) * 1.0 / np.sqrt(C) * fc[:, None] / fd, "e2m1")
    oldsp = pack_weight(n((C, Z)) / fc[:, None], "e4m3")
    return {
        "wp_words": wpp[0],
        "wp_scales": wpp[1],
        "olds_words": oldsp[0],
        "olds_scales": oldsp[1],
        "query": (n((D, Q)) * 1.0 / np.sqrt(D) * fd[:, None]).astype(np.float32),
        "offs": striped8(idx),
        "offs2": striped8(idx2),
        "offs3": striped8(idx3),
        "offs4": striped8(idx4),
        "offs5": striped8(idx5),
    }


def reference(wp_words, wp_scales, olds_words, olds_scales, query, offs, offs2, offs3, offs4, offs5):
    idx = unstriped8(offs)
    idx2 = unstriped8(offs2)
    idx3 = unstriped8(offs3)
    idx4 = unstriped8(offs4)
    idx5 = unstriped8(offs5)
    wpu = unpack_weight(wp_words, wp_scales, "e2m1")
    oldsu = unpack_weight(olds_words, olds_scales, "e4m3")
    kb = wpu.T @ oldsu
    f1 = np.zeros((D, Z))
    f1[np.arange(D)[:, None], idx2[np.arange(D) % 512 // 64]] = pick8(kb, idx, 64)
    pg = kb - f1
    queryq = mxq(f64(query), 0, "e4m3")
    pgq = mxq(pg, 0, "e4m3")
    s = queryq.T @ pgq
    f2 = np.zeros((Q, Z))
    f2[np.arange(Q)[:, None], idx4[np.arange(Q) % 128 // 16]] = pick8(s, idx3, 16)
    ss = s + f2
    y = np.maximum(pick8(ss, idx5, 16), pick8(s, idx3, 16))
    return y

@@ -1,0 +1,227 @@
+from contextlib import ExitStack
+
+import concourse.mybir as mybir
+
+C, D, Z, Q, PICKS = 512, 512, 512, 128, 256
+FLOPS = 2 * C * D * Z + 2 * D * Q * Z
+
+F32 = mybir.dt.float32
+BF16 = mybir.dt.bfloat16
+I32 = mybir.dt.int32
+U32 = mybir.dt.uint32
+U16 = mybir.dt.uint16
+U8 = mybir.dt.uint8
+FP8X4 = mybir.dt.float8_e4m3fn_x4
+FP4X4 = mybir.dt.float4_e2m1fn_x4
+COPY = mybir.ActivationFunctionType.Copy
+ALU = mybir.AluOpType
+
+P = 128
+PACK = 4
+HALF = Z // 2
+LIST_COLS = PICKS // 16
+HALF_PICKS = PICKS // 2
+PIECES = 4
+PIECE = Z // PIECES
+
+
+def tile_attend_headmoves_plainq_kernel(
+    tc, wp_words, wp_scales, olds_words, olds_scales, query, offs, offs2, offs3, offs4, offs5, out
+):
+    nc = tc.nc
+    with ExitStack() as ctx:
+        lists = ctx.enter_context(tc.tile_pool(name="lists", bufs=1))
+        sb = ctx.enter_context(tc.tile_pool(name="sb", bufs=1))
+        shared = ctx.enter_context(tc.tile_pool(name="shared", bufs=1))
+        psum = ctx.enter_context(tc.psum_pool(name="psum", bufs=1))
+
+        def load_list(name, source):
+            tile = lists.tile([P, LIST_COLS], U16, name=name)
+            nc.sync.dma_start(tile[:], source)
+            return tile
+
+        def list_half(tile, h):
+            return tile[:, h * LIST_COLS // 2 : (h + 1) * LIST_COLS // 2]
+
+        wp_rows = sb.tile([P, 2 * D], U8, align_bytes=64)
+        olds_rows = sb.tile([P, 2 * Z], U8, align_bytes=64)
+        nc.vector.memset(wp_rows[:].bitcast(I32), 0)
+        nc.gpsimd.memset(olds_rows[:].bitcast(I32), 0)
+
+        olds_codes = sb.tile([P, Z], U32, align_bytes=64)
+        nc.scalar.dma_start(
+            olds_codes[:].bitcast(I32), olds_words[0].rearrange("p n t -> p (n t)").bitcast(I32)
+        )
+        wp_raw = sb.tile([P, 2 * D], U8, tag="staged")
+        nc.sync.dma_start(wp_raw[:].bitcast(I32), wp_words[0].bitcast(I32))
+        idx = load_list("idx", offs)
+        idx2 = load_list("idx2", offs2)
+
+        for rows, scales in ((wp_rows, wp_scales), (olds_rows, olds_scales)):
+            source = scales[0].bitcast(I32).rearrange("(h g r) w -> g r h w", h=2, g=2)
+            for g in range(2):
+                target = rows[32 * g : 32 * g + 4, :].bitcast(I32).rearrange("r (h w) -> r h w", h=2)
+                nc.sync.dma_start(target, source[g])
+
+        idx3 = load_list("idx3", offs3)
+        idx4 = load_list("idx4", offs4)
+        idx5 = load_list("idx5", offs5)
+
+        f1 = [sb.tile([P, Z], F32, name="f1_%d" % t) for t in range(PACK - 1)]
+        f2 = [sb.tile([P, Z], F32, name="f2_0")]
+        for window in f1[0:2]:
+            nc.vector.memset(window[:], 0.0)
+        for window in (f1[2], f2[0]):
+            nc.gpsimd.memset(window[:], 0.0)
+        f1.append(f1[0])
+
+        wp_codes = sb.tile([P, 2 * D], U8, align_bytes=64)
+        nc.vector.tensor_copy(
+            wp_codes[:].bitcast(U16).rearrange("p (t m) -> p t m", t=PACK),
+            wp_raw[:].bitcast(U16).rearrange("p (m t) -> p t m", t=PACK),
+        )
+        q_raw = sb.tile([P, PACK, Q], F32, tag="staged")
+        nc.sync.dma_start(q_raw[:], query.rearrange("(p t) q -> p t q", t=PACK))
+
+        for rows in (wp_rows, olds_rows):
+            words = rows[:].bitcast(I32)
+            nc.vector.tensor_copy(words[64:128, 0 : D // 4], words[0:64, D // 4 : D // 2])
+
+        wp_plane = [sb.tile([P, P], U8, align_bytes=64, name="wp_plane_0"),
+                    sb.tile([P, 3 * P], U8, align_bytes=64, name="wp_plane_rest")]
+        dealt_bytes = wp_rows[:, 0:D].rearrange("p (m t) -> p t m", t=PACK)
+        nc.vector.tensor_copy(wp_plane[0][:], dealt_bytes[:, 0, :])
+        nc.vector.tensor_copy(
+            wp_plane[1][:].rearrange("p (t m) -> p t m", t=3), dealt_bytes[:, 1:PACK, :]
+        )
+
+        def keys_matmul(bank, t, cols):
+            part, j = (0, 0) if t == 0 else (1, t - 1)
+            nc.tensor.matmul_mx(
+                out=bank[:],
+                lhsT=wp_codes[:, 2 * P * t : 2 * P * (t + 1)].bitcast(FP4X4),
+                lhsT_scale=wp_plane[part][:, P * j : P * (j + 1)],
+                rhs=olds_codes[:, cols].bitcast(FP8X4),
+                rhs_scale=olds_rows[:, cols],
+                start=True,
+                stop=True,
+            )
+
+        halves = [slice(h * HALF, (h + 1) * HALF) for h in range(2)]
+        pick_halves = [slice(h * HALF_PICKS, (h + 1) * HALF_PICKS) for h in range(2)]
+        kb = [sb.tile([P, Z], F32, name="kb_%d" % t, tag="kb_%d" % t, align_bytes=64) for t in range(2)]
+        kb = kb + [shared.tile([P, Z], F32, name="kb_%d" % t, offset=4 * Z * (t - 2)) for t in range(2, PACK)]
+        picked = [sb.tile([P, PICKS], F32, name="picked_%d" % t, tag="picked_%d" % t) for t in range(PACK)]
+
+        pieces = [slice(k * PIECE, (k + 1) * PIECE) for k in range(PIECES)]
+        for k, tag in enumerate(("scores_0", "scores_1", "scores_2", "chain")):
+            bank_0 = psum.tile([P, PIECE], F32, tag=tag)
+            keys_matmul(bank_0, 0, pieces[k])
+            if k % 2 == 0:
+                nc.vector.tensor_copy(kb[0][:, pieces[k]], bank_0[:])
+            else:
+                nc.scalar.activation(kb[0][:, pieces[k]], bank_0[:], COPY)
+        bank_1a = psum.tile([P, HALF], F32, tag="side")
+        keys_matmul(bank_1a, 1, halves[0])
+        nc.scalar.activation(kb[1][:, halves[0]], bank_1a[:], COPY)
+        for h in range(2):
+            nc.vector.tensor_copy(picked[0][:, pick_halves[h]], kb[0][:].indirect(list_half(idx, h)))
+            nc.scalar.activation(
+                f1[0][:].indirect(list_half(idx2, h)), picked[0][:, pick_halves[h]], COPY
+            )
+
+        for k, tag in ((2, "chain"), (3, "side")):
+            bank_1b = psum.tile([P, PIECE], F32, tag=tag)
+            keys_matmul(bank_1b, 1, pieces[k])
+            nc.vector.tensor_copy(kb[1][:, pieces[k]], bank_1b[:])
+
+        def pick_keys(t):
+            nc.vector.tensor_copy(picked[t][:], kb[t][:].indirect(idx[:]))
+
+        def place_keys(t):
+            nc.scalar.activation(f1[t][:].indirect(idx2[:]), picked[t][:], COPY)
+
+        pick_keys(1)
+        place_keys(1)
+        bank_2 = psum.tile([P, Z], F32, tag="chain")
+        bank_3 = psum.tile([P, Z], F32, tag="side")
+        for t, bank in ((2, bank_2), (3, bank_3)):
+            keys_matmul(bank, t, slice(0, Z))
+            nc.vector.tensor_copy(kb[t][:], bank[:])
+        pick_keys(2)
+        place_keys(2)
+        pick_keys(3)
+
+        q_grouped = sb.tile([P, Q, PACK], BF16, tag="kb_0", align_bytes=64)
+        pairs = shared.tile([P, PIECES, 2, PIECE, 2], BF16, offset=0)
+        keys = [kb[0], kb[1], bank_2, bank_3]
+        q_codes = sb.tile([P, Q], U32, align_bytes=64)
+        q_plane = sb.tile([P, Q], U8, align_bytes=64)
+        for t in range(PACK - 1):
+            nc.vector.tensor_tensor(
+                pairs[:, :, t // 2, :, t % 2],
+                keys[t][:].rearrange("p (k z) -> p k z", k=PIECES),
+                f1[t][:].rearrange("p (k z) -> p k z", k=PIECES),
+                ALU.subtract,
+            )
+            if t == 0:
+                place_keys(3)
+                f2.append(sb.tile([P, Z], F32, name="f2_1", tag="picked_3"))
+                nc.gpsimd.memset(f2[1][:], 0.0)
+                nc.vector.tensor_copy(q_grouped[:], q_raw[:].rearrange("p t q -> p q t"))
+            if t == 1:
+                nc.vector.quantize_mx(
+                    q_codes[:].bitcast(FP8X4), q_plane[:], q_grouped[:].rearrange("p q t -> p (q t)")
+                )
+
+        for k in range(PIECES):
+            nc.vector.tensor_tensor(
+                pairs[:, k, 1, :, 1], bank_3[:, pieces[k]], f1[PACK - 1][:, pieces[k]], ALU.subtract
+            )
+
+        s = sb.tile([P, Z], F32)
+        for k in range(PIECES):
+            grouped = sb.tile([P, PIECE * PACK], BF16, name="grouped_%d" % k, align_bytes=64)
+            target = grouped[:].bitcast(F32).rearrange("p (z u) -> p z u", u=2)
+            source = pairs[:, k].rearrange("p u z e -> p (u z e)").bitcast(F32).rearrange("p (u z) -> p z u", u=2)
+            if k < PIECES - 1:
+                nc.scalar.copy(target, source)
+            else:
+                nc.vector.tensor_copy(target, source)
+            pg_codes = sb.tile([P, PIECE], U32, name="pg_codes_%d" % k, align_bytes=64)
+            pg_plane = sb.tile([P, PIECE], U8, name="pg_plane_%d" % k, align_bytes=64)
+            nc.vector.quantize_mx(pg_codes[:].bitcast(FP8X4), pg_plane[:], grouped[:])
+            scores = psum.tile([P, PIECE], F32, name="scores_%d" % k, tag="scores_%d" % k)
+            nc.tensor.matmul_mx(
+                out=scores[:],
+                lhsT=q_codes[:].bitcast(FP8X4),
+                lhsT_scale=q_plane[:],
+                rhs=pg_codes[:].bitcast(FP8X4),
+                rhs_scale=pg_plane[:],
+                start=True,
+                stop=True,
+            )
+            if k < PIECES - 1:
+                nc.scalar.activation(s[:, pieces[k]], scores[:], COPY)
+            else:
+                nc.vector.tensor_copy(s[:, pieces[k]], scores[:])
+
+        s_picked = sb.tile([P, PICKS], F32)
+        for h in range(2):
+            nc.vector.tensor_copy(s_picked[:, pick_halves[h]], s[:].indirect(list_half(idx3, h)))
+            nc.scalar.activation(
+                f2[h][:].indirect(list_half(idx4, h)), s_picked[:, pick_halves[h]], COPY
+            )
+
+        partial = sb.tile([P, Z], F32)
+        nc.vector.tensor_tensor(partial[:], s[:], f2[0][:], ALU.add)
+        ss = sb.tile([P, Z], F32)
+        nc.vector.tensor_tensor(ss[:], partial[:], f2[1][:], ALU.add)
+        ss_picked = sb.tile([P, PICKS], F32)
+        nc.vector.tensor_copy(ss_picked[:, pick_halves[0]], ss[:].indirect(list_half(idx5, 0)))
+        nc.scalar.activation(ss_picked[:, pick_halves[1]], ss[:].indirect(list_half(idx5, 1)), COPY)
+        y = sb.tile([P, PICKS], F32)
+        for h, queue in ((0, nc.sync), (1, nc.scalar)):
+            cols = pick_halves[h]
+            nc.vector.tensor_tensor(y[:, cols], ss_picked[:, cols], s_picked[:, cols], ALU.max)
+            queue.dma_start(out[:, cols], y[:, cols])

@@ -48,21 +48,23 @@ def tile_attend_headmoves_plainq_kernel(
         nc.vector.memset(wp_rows[:].bitcast(I32), 0)
         nc.gpsimd.memset(olds_rows[:].bitcast(I32), 0)
 
-        olds_codes = sb.tile([P, Z], U32, align_bytes=64)
-        nc.scalar.dma_start(
-            olds_codes[:].bitcast(I32), olds_words[0].rearrange("p n t -> p (n t)").bitcast(I32)
-        )
-        wp_raw = sb.tile([P, 2 * D], U8, tag="staged")
-        nc.sync.dma_start(wp_raw[:].bitcast(I32), wp_words[0].bitcast(I32))
+        wp_raw = sb.tile([P, 2 * D], U8)
+        nc.scalar.dma_start(wp_raw[:].bitcast(I32), wp_words[0].bitcast(I32))
         idx = load_list("idx", offs)
-        idx2 = load_list("idx2", offs2)
 
-        for rows, scales in ((wp_rows, wp_scales), (olds_rows, olds_scales)):
+        for rows, scales, queue in ((wp_rows, wp_scales, nc.sync), (olds_rows, olds_scales, nc.scalar)):
             source = scales[0].bitcast(I32).rearrange("(h g r) w -> g r h w", h=2, g=2)
             for g in range(2):
                 target = rows[32 * g : 32 * g + 4, :].bitcast(I32).rearrange("r (h w) -> r h w", h=2)
-                nc.sync.dma_start(target, source[g])
+                queue.dma_start(target, source[g])
 
+        olds_codes = sb.tile([P, Z], U32, align_bytes=64)
+        nc.sync.dma_start(
+            olds_codes[:].bitcast(I32), olds_words[0].rearrange("p n t -> p (n t)").bitcast(I32)
+        )
+        q_raw = sb.tile([P, PACK, Q], F32)
+        nc.sync.dma_start(q_raw[:], query.rearrange("(p t) q -> p t q", t=PACK))
+        idx2 = load_list("idx2", offs2)
         idx3 = load_list("idx3", offs3)
         idx4 = load_list("idx4", offs4)
         idx5 = load_list("idx5", offs5)
@@ -80,20 +82,20 @@ def tile_attend_headmoves_plainq_kernel(
             wp_codes[:].bitcast(U16).rearrange("p (t m) -> p t m", t=PACK),
             wp_raw[:].bitcast(U16).rearrange("p (m t) -> p t m", t=PACK),
         )
-        q_raw = sb.tile([P, PACK, Q], F32, tag="staged")
-        nc.sync.dma_start(q_raw[:], query.rearrange("(p t) q -> p t q", t=PACK))
 
         for rows in (wp_rows, olds_rows):
             words = rows[:].bitcast(I32)
             nc.vector.tensor_copy(words[64:128, 0 : D // 4], words[0:64, D // 4 : D // 2])
 
         wp_plane = [sb.tile([P, P], U8, align_bytes=64, name="wp_plane_0"),
-                    sb.tile([P, 3 * P], U8, align_bytes=64, name="wp_plane_rest")]
+                    sb.tile([P, 3 * P], U8, align_bytes=64, name="wp_plane_rest", tag="plane")]
         dealt_bytes = wp_rows[:, 0:D].rearrange("p (m t) -> p t m", t=PACK)
         nc.vector.tensor_copy(wp_plane[0][:], dealt_bytes[:, 0, :])
         nc.vector.tensor_copy(
             wp_plane[1][:].rearrange("p (t m) -> p t m", t=3), dealt_bytes[:, 1:PACK, :]
         )
+        q_grouped = sb.tile([P, Q, PACK], BF16, align_bytes=64)
+        nc.vector.tensor_copy(q_grouped[:], q_raw[:].rearrange("p t q -> p q t"))
 
         def keys_matmul(bank, t, cols):
             part, j = (0, 0) if t == 0 else (1, t - 1)
@@ -152,11 +154,13 @@ def tile_attend_headmoves_plainq_kernel(
         place_keys(2)
         pick_keys(3)
 
-        q_grouped = sb.tile([P, Q, PACK], BF16, tag="kb_0", align_bytes=64)
         pairs = shared.tile([P, PIECES, 2, PIECE, 2], BF16, offset=0)
         keys = [kb[0], kb[1], bank_2, bank_3]
         q_codes = sb.tile([P, Q], U32, align_bytes=64)
-        q_plane = sb.tile([P, Q], U8, align_bytes=64)
+        q_plane = sb.tile([P, Q], U8, align_bytes=64, tag="plane")
+        nc.vector.quantize_mx(
+            q_codes[:].bitcast(FP8X4), q_plane[:], q_grouped[:].rearrange("p q t -> p (q t)")
+        )
         for t in range(PACK - 1):
             nc.vector.tensor_tensor(
                 pairs[:, :, t // 2, :, t % 2],
@@ -168,11 +172,6 @@ def tile_attend_headmoves_plainq_kernel(
                 place_keys(3)
                 f2.append(sb.tile([P, Z], F32, name="f2_1", tag="picked_3"))
                 nc.gpsimd.memset(f2[1][:], 0.0)
-                nc.vector.tensor_copy(q_grouped[:], q_raw[:].rearrange("p t q -> p q t"))
-            if t == 1:
-                nc.vector.quantize_mx(
-                    q_codes[:].bitcast(FP8X4), q_plane[:], q_grouped[:].rearrange("p q t -> p (q t)")
-                )
 
         for k in range(PIECES):
             nc.vector.tensor_tensor(

@@ -116,26 +116,21 @@ def tile_attend_headmoves_plainq_kernel(
         picked = [sb.tile([P, PICKS], F32, name="picked_%d" % t, tag="picked_%d" % t) for t in range(PACK)]
 
         pieces = [slice(k * PIECE, (k + 1) * PIECE) for k in range(PIECES)]
-        for k, tag in enumerate(("scores_0", "scores_1", "scores_2", "chain")):
+        for k, tag in enumerate(("scores_0", "chain", "scores_1", "side")):
             bank_0 = psum.tile([P, PIECE], F32, tag=tag)
             keys_matmul(bank_0, 0, pieces[k])
             if k % 2 == 0:
                 nc.vector.tensor_copy(kb[0][:, pieces[k]], bank_0[:])
             else:
                 nc.scalar.activation(kb[0][:, pieces[k]], bank_0[:], COPY)
-        bank_1a = psum.tile([P, HALF], F32, tag="side")
-        keys_matmul(bank_1a, 1, halves[0])
-        nc.scalar.activation(kb[1][:, halves[0]], bank_1a[:], COPY)
-        for h in range(2):
-            nc.vector.tensor_copy(picked[0][:, pick_halves[h]], kb[0][:].indirect(list_half(idx, h)))
-            nc.scalar.activation(
-                f1[0][:].indirect(list_half(idx2, h)), picked[0][:, pick_halves[h]], COPY
-            )
+        nc.vector.tensor_copy(picked[0][:, pick_halves[0]], kb[0][:].indirect(list_half(idx, 0)))
+        nc.scalar.activation(picked[0][:, pick_halves[1]], kb[0][:].indirect(list_half(idx, 1)), COPY)
+        nc.scalar.activation(f1[0][:].indirect(idx2[:]), picked[0][:], COPY)
 
-        for k, tag in ((2, "chain"), (3, "side")):
-            bank_1b = psum.tile([P, PIECE], F32, tag=tag)
-            keys_matmul(bank_1b, 1, pieces[k])
-            nc.vector.tensor_copy(kb[1][:, pieces[k]], bank_1b[:])
+        for h, tag in enumerate(("chain", "side")):
+            bank_1 = psum.tile([P, HALF], F32, tag=tag)
+            keys_matmul(bank_1, 1, halves[h])
+            nc.vector.tensor_copy(kb[1][:, halves[h]], bank_1[:])
 
         def pick_keys(t):
             nc.vector.tensor_copy(picked[t][:], kb[t][:].indirect(idx[:]))
@@ -154,7 +149,7 @@ def tile_attend_headmoves_plainq_kernel(
         place_keys(2)
         pick_keys(3)
 
-        pairs = shared.tile([P, PIECES, 2, PIECE, 2], BF16, offset=0)
+        planes = shared.tile([P, PIECES, PACK, PIECE], BF16, offset=0)
         keys = [kb[0], kb[1], bank_2, bank_3]
         q_codes = sb.tile([P, Q], U32, align_bytes=64)
         q_plane = sb.tile([P, Q], U8, align_bytes=64, tag="plane")
@@ -163,7 +158,7 @@ def tile_attend_headmoves_plainq_kernel(
         )
         for t in range(PACK - 1):
             nc.vector.tensor_tensor(
-                pairs[:, :, t // 2, :, t % 2],
+                planes[:, :, t, :],
                 keys[t][:].rearrange("p (k z) -> p k z", k=PIECES),
                 f1[t][:].rearrange("p (k z) -> p k z", k=PIECES),
                 ALU.subtract,
@@ -175,15 +170,15 @@ def tile_attend_headmoves_plainq_kernel(
 
         for k in range(PIECES):
             nc.vector.tensor_tensor(
-                pairs[:, k, 1, :, 1], bank_3[:, pieces[k]], f1[PACK - 1][:, pieces[k]], ALU.subtract
+                planes[:, k, PACK - 1, :], bank_3[:, pieces[k]], f1[PACK - 1][:, pieces[k]], ALU.subtract
             )
 
         s = sb.tile([P, Z], F32)
         for k in range(PIECES):
             grouped = sb.tile([P, PIECE * PACK], BF16, name="grouped_%d" % k, align_bytes=64)
-            target = grouped[:].bitcast(F32).rearrange("p (z u) -> p z u", u=2)
-            source = pairs[:, k].rearrange("p u z e -> p (u z e)").bitcast(F32).rearrange("p (u z) -> p z u", u=2)
-            if k < PIECES - 1:
+            target = grouped[:].rearrange("p (c i t) -> p c t i", i=4, t=PACK)
+            source = planes[:, k].rearrange("p t (c i) -> p c t i", i=4)
+            if k < 2:
                 nc.scalar.copy(target, source)
             else:
                 nc.vector.tensor_copy(target, source)

@@ -69,13 +69,12 @@ def tile_attend_headmoves_plainq_kernel(
         idx4 = load_list("idx4", offs4)
         idx5 = load_list("idx5", offs5)
 
-        f1 = [sb.tile([P, Z], F32, name="f1_%d" % t) for t in range(PACK - 1)]
+        f1 = [sb.tile([P, Z], F32, name="f1_%d" % t) for t in range(PACK)]
         f2 = [sb.tile([P, Z], F32, name="f2_0")]
-        for window in f1[0:2]:
+        for window in f1[0:3]:
             nc.vector.memset(window[:], 0.0)
-        for window in (f1[2], f2[0]):
+        for window in (f1[3], f2[0]):
             nc.gpsimd.memset(window[:], 0.0)
-        f1.append(f1[0])
 
         wp_codes = sb.tile([P, 2 * D], U8, align_bytes=64)
         nc.vector.tensor_copy(
@@ -149,36 +148,36 @@ def tile_attend_headmoves_plainq_kernel(
         place_keys(2)
         pick_keys(3)
 
-        planes = shared.tile([P, PIECES, PACK, PIECE], BF16, offset=0)
+        pairs = shared.tile([P, PIECES, 2, PIECE, 2], BF16, offset=0)
         keys = [kb[0], kb[1], bank_2, bank_3]
         q_codes = sb.tile([P, Q], U32, align_bytes=64)
         q_plane = sb.tile([P, Q], U8, align_bytes=64, tag="plane")
         nc.vector.quantize_mx(
             q_codes[:].bitcast(FP8X4), q_plane[:], q_grouped[:].rearrange("p q t -> p (q t)")
         )
+        place_keys(3)
+        f2.append(sb.tile([P, Z], F32, name="f2_1", tag="picked_3"))
         for t in range(PACK - 1):
-            nc.vector.tensor_tensor(
-                planes[:, :, t, :],
+            engine = nc.gpsimd if t < 2 else nc.vector
+            engine.tensor_tensor(
+                pairs[:, :, t // 2, :, t % 2],
                 keys[t][:].rearrange("p (k z) -> p k z", k=PIECES),
                 f1[t][:].rearrange("p (k z) -> p k z", k=PIECES),
                 ALU.subtract,
             )
-            if t == 0:
-                place_keys(3)
-                f2.append(sb.tile([P, Z], F32, name="f2_1", tag="picked_3"))
-                nc.gpsimd.memset(f2[1][:], 0.0)
+        nc.gpsimd.memset(f2[1][:], 0.0)
 
         for k in range(PIECES):
             nc.vector.tensor_tensor(
-                planes[:, k, PACK - 1, :], bank_3[:, pieces[k]], f1[PACK - 1][:, pieces[k]], ALU.subtract
+                pairs[:, k, 1, :, 1], bank_3[:, pieces[k]], f1[PACK - 1][:, pieces[k]], ALU.subtract
             )
 
         s = sb.tile([P, Z], F32)
         for k in range(PIECES):
             grouped = sb.tile([P, PIECE * PACK], BF16, name="grouped_%d" % k, align_bytes=64)
-            target = grouped[:].rearrange("p (c i t) -> p c t i", i=4, t=PACK)
-            source = planes[:, k].rearrange("p t (c i) -> p c t i", i=4)
-            if k < 2:
+            target = grouped[:].bitcast(F32).rearrange("p (z u) -> p z u", u=2)
+            source = pairs[:, k].rearrange("p u z e -> p (u z e)").bitcast(F32).rearrange("p (u z) -> p z u", u=2)
+            if k < PIECES - 1:
                 nc.scalar.copy(target, source)
             else:
                 nc.vector.tensor_copy(target, source)

from contextlib import ExitStack

import concourse.mybir as mybir

C, D, Z, Q, PICKS = 512, 512, 512, 128, 256
FLOPS = 2 * C * D * Z + 2 * D * Q * Z

F32 = mybir.dt.float32
BF16 = mybir.dt.bfloat16
I32 = mybir.dt.int32
U32 = mybir.dt.uint32
U16 = mybir.dt.uint16
U8 = mybir.dt.uint8
FP8X4 = mybir.dt.float8_e4m3fn_x4
FP4X4 = mybir.dt.float4_e2m1fn_x4
COPY = mybir.ActivationFunctionType.Copy
ALU = mybir.AluOpType

P = 128
PACK = 4
HALF = Z // 2
LIST_COLS = PICKS // 16
HALF_PICKS = PICKS // 2
PIECES = 4
PIECE = Z // PIECES


def tile_attend_headmoves_plainq_kernel(
    tc, wp_words, wp_scales, olds_words, olds_scales, query, offs, offs2, offs3, offs4, offs5, out
):
    nc = tc.nc
    with ExitStack() as ctx:
        lists = ctx.enter_context(tc.tile_pool(name="lists", bufs=1))
        sb = ctx.enter_context(tc.tile_pool(name="sb", bufs=1))
        shared = ctx.enter_context(tc.tile_pool(name="shared", bufs=1))
        psum = ctx.enter_context(tc.psum_pool(name="psum", bufs=1))

        def load_list(name, source):
            tile = lists.tile([P, LIST_COLS], U16, name=name)
            nc.sync.dma_start(tile[:], source)
            return tile

        def list_half(tile, h):
            return tile[:, h * LIST_COLS // 2 : (h + 1) * LIST_COLS // 2]

        wp_rows = sb.tile([P, 2 * D], U8, align_bytes=64)
        olds_rows = sb.tile([P, 2 * Z], U8, align_bytes=64)
        nc.vector.memset(wp_rows[:].bitcast(I32), 0)
        nc.gpsimd.memset(olds_rows[:].bitcast(I32), 0)

        wp_raw = sb.tile([P, 2 * D], U8)
        nc.scalar.dma_start(wp_raw[:].bitcast(I32), wp_words[0].bitcast(I32))
        idx = load_list("idx", offs)

        for rows, scales, queue in ((wp_rows, wp_scales, nc.sync), (olds_rows, olds_scales, nc.scalar)):
            source = scales[0].bitcast(I32).rearrange("(h g r) w -> g r h w", h=2, g=2)
            for g in range(2):
                target = rows[32 * g : 32 * g + 4, :].bitcast(I32).rearrange("r (h w) -> r h w", h=2)
                queue.dma_start(target, source[g])

        olds_codes = sb.tile([P, Z], U32, align_bytes=64)
        nc.sync.dma_start(
            olds_codes[:].bitcast(I32), olds_words[0].rearrange("p n t -> p (n t)").bitcast(I32)
        )
        q_raw = sb.tile([P, PACK, Q], F32)
        nc.sync.dma_start(q_raw[:], query.rearrange("(p t) q -> p t q", t=PACK))
        idx2 = load_list("idx2", offs2)
        idx3 = load_list("idx3", offs3)
        idx4 = load_list("idx4", offs4)
        idx5 = load_list("idx5", offs5)

        f1 = [sb.tile([P, Z], F32, name="f1_%d" % t) for t in range(PACK)]
        f2 = [sb.tile([P, Z], F32, name="f2_0")]
        for window in f1[0:3]:
            nc.vector.memset(window[:], 0.0)
        for window in (f1[3], f2[0]):
            nc.gpsimd.memset(window[:], 0.0)

        wp_codes = sb.tile([P, 2 * D], U8, align_bytes=64)
        nc.vector.tensor_copy(
            wp_codes[:].bitcast(U16).rearrange("p (t m) -> p t m", t=PACK),
            wp_raw[:].bitcast(U16).rearrange("p (m t) -> p t m", t=PACK),
        )

        for rows in (wp_rows, olds_rows):
            words = rows[:].bitcast(I32)
            nc.vector.tensor_copy(words[64:128, 0 : D // 4], words[0:64, D // 4 : D // 2])

        wp_plane = [sb.tile([P, P], U8, align_bytes=64, name="wp_plane_0"),
                    sb.tile([P, 3 * P], U8, align_bytes=64, name="wp_plane_rest", tag="plane")]
        dealt_bytes = wp_rows[:, 0:D].rearrange("p (m t) -> p t m", t=PACK)
        nc.vector.tensor_copy(wp_plane[0][:], dealt_bytes[:, 0, :])
        nc.vector.tensor_copy(
            wp_plane[1][:].rearrange("p (t m) -> p t m", t=3), dealt_bytes[:, 1:PACK, :]
        )
        q_grouped = sb.tile([P, Q, PACK], BF16, align_bytes=64)
        nc.vector.tensor_copy(q_grouped[:], q_raw[:].rearrange("p t q -> p q t"))

        def keys_matmul(bank, t, cols):
            part, j = (0, 0) if t == 0 else (1, t - 1)
            nc.tensor.matmul_mx(
                out=bank[:],
                lhsT=wp_codes[:, 2 * P * t : 2 * P * (t + 1)].bitcast(FP4X4),
                lhsT_scale=wp_plane[part][:, P * j : P * (j + 1)],
                rhs=olds_codes[:, cols].bitcast(FP8X4),
                rhs_scale=olds_rows[:, cols],
                start=True,
                stop=True,
            )

        halves = [slice(h * HALF, (h + 1) * HALF) for h in range(2)]
        pick_halves = [slice(h * HALF_PICKS, (h + 1) * HALF_PICKS) for h in range(2)]
        kb = [sb.tile([P, Z], F32, name="kb_%d" % t, tag="kb_%d" % t, align_bytes=64) for t in range(2)]
        kb = kb + [shared.tile([P, Z], F32, name="kb_%d" % t, offset=4 * Z * (t - 2)) for t in range(2, PACK)]
        picked = [sb.tile([P, PICKS], F32, name="picked_%d" % t, tag="picked_%d" % t) for t in range(PACK)]

        pieces = [slice(k * PIECE, (k + 1) * PIECE) for k in range(PIECES)]
        for k, tag in enumerate(("scores_0", "chain", "scores_1", "side")):
            bank_0 = psum.tile([P, PIECE], F32, tag=tag)
            keys_matmul(bank_0, 0, pieces[k])
            if k % 2 == 0:
                nc.vector.tensor_copy(kb[0][:, pieces[k]], bank_0[:])
            else:
                nc.scalar.activation(kb[0][:, pieces[k]], bank_0[:], COPY)
        nc.vector.tensor_copy(picked[0][:, pick_halves[0]], kb[0][:].indirect(list_half(idx, 0)))
        nc.scalar.activation(picked[0][:, pick_halves[1]], kb[0][:].indirect(list_half(idx, 1)), COPY)
        nc.scalar.activation(f1[0][:].indirect(idx2[:]), picked[0][:], COPY)

        for h, tag in enumerate(("chain", "side")):
            bank_1 = psum.tile([P, HALF], F32, tag=tag)
            keys_matmul(bank_1, 1, halves[h])
            nc.vector.tensor_copy(kb[1][:, halves[h]], bank_1[:])

        def pick_keys(t):
            nc.vector.tensor_copy(picked[t][:], kb[t][:].indirect(idx[:]))

        def place_keys(t):
            nc.scalar.activation(f1[t][:].indirect(idx2[:]), picked[t][:], COPY)

        pick_keys(1)
        place_keys(1)
        bank_2 = psum.tile([P, Z], F32, tag="chain")
        bank_3 = psum.tile([P, Z], F32, tag="side")
        for t, bank in ((2, bank_2), (3, bank_3)):
            keys_matmul(bank, t, slice(0, Z))
            nc.vector.tensor_copy(kb[t][:], bank[:])
        pick_keys(2)
        place_keys(2)
        pick_keys(3)

        pairs = shared.tile([P, PIECES, 2, PIECE, 2], BF16, offset=0)
        keys = [kb[0], kb[1], bank_2, bank_3]
        q_codes = sb.tile([P, Q], U32, align_bytes=64)
        q_plane = sb.tile([P, Q], U8, align_bytes=64, tag="plane")
        nc.vector.quantize_mx(
            q_codes[:].bitcast(FP8X4), q_plane[:], q_grouped[:].rearrange("p q t -> p (q t)")
        )
        place_keys(3)
        f2.append(sb.tile([P, Z], F32, name="f2_1", tag="picked_3"))
        for t in range(PACK - 1):
            engine = nc.gpsimd if t < 2 else nc.vector
            engine.tensor_tensor(
                pairs[:, :, t // 2, :, t % 2],
                keys[t][:].rearrange("p (k z) -> p k z", k=PIECES),
                f1[t][:].rearrange("p (k z) -> p k z", k=PIECES),
                ALU.subtract,
            )
        nc.gpsimd.memset(f2[1][:], 0.0)

        for k in range(PIECES):
            nc.vector.tensor_tensor(
                pairs[:, k, 1, :, 1], bank_3[:, pieces[k]], f1[PACK - 1][:, pieces[k]], ALU.subtract
            )

        s = sb.tile([P, Z], F32)
        for k in range(PIECES):
            grouped = sb.tile([P, PIECE * PACK], BF16, name="grouped_%d" % k, align_bytes=64)
            target = grouped[:].bitcast(F32).rearrange("p (z u) -> p z u", u=2)
            source = pairs[:, k].rearrange("p u z e -> p (u z e)").bitcast(F32).rearrange("p (u z) -> p z u", u=2)
            if k < PIECES - 1:
                nc.scalar.copy(target, source)
            else:
                nc.vector.tensor_copy(target, source)
            pg_codes = sb.tile([P, PIECE], U32, name="pg_codes_%d" % k, align_bytes=64)
            pg_plane = sb.tile([P, PIECE], U8, name="pg_plane_%d" % k, align_bytes=64)
            nc.vector.quantize_mx(pg_codes[:].bitcast(FP8X4), pg_plane[:], grouped[:])
            scores = psum.tile([P, PIECE], F32, name="scores_%d" % k, tag="scores_%d" % k)
            nc.tensor.matmul_mx(
                out=scores[:],
                lhsT=q_codes[:].bitcast(FP8X4),
                lhsT_scale=q_plane[:],
                rhs=pg_codes[:].bitcast(FP8X4),
                rhs_scale=pg_plane[:],
                start=True,
                stop=True,
            )
            if k < PIECES - 1:
                nc.scalar.activation(s[:, pieces[k]], scores[:], COPY)
            else:
                nc.vector.tensor_copy(s[:, pieces[k]], scores[:])

        s_picked = sb.tile([P, PICKS], F32)
        for h in range(2):
            nc.vector.tensor_copy(s_picked[:, pick_halves[h]], s[:].indirect(list_half(idx3, h)))
            nc.scalar.activation(
                f2[h][:].indirect(list_half(idx4, h)), s_picked[:, pick_halves[h]], COPY
            )

        partial = sb.tile([P, Z], F32)
        nc.vector.tensor_tensor(partial[:], s[:], f2[0][:], ALU.add)
        ss = sb.tile([P, Z], F32)
        nc.vector.tensor_tensor(ss[:], partial[:], f2[1][:], ALU.add)
        ss_picked = sb.tile([P, PICKS], F32)
        nc.vector.tensor_copy(ss_picked[:, pick_halves[0]], ss[:].indirect(list_half(idx5, 0)))
        nc.scalar.activation(ss_picked[:, pick_halves[1]], ss[:].indirect(list_half(idx5, 1)), COPY)
        y = sb.tile([P, PICKS], F32)
        for h, queue in ((0, nc.sync), (1, nc.scalar)):
            cols = pick_halves[h]
            nc.vector.tensor_tensor(y[:, cols], ss_picked[:, cols], s_picked[:, cols], ALU.max)
            queue.dma_start(out[:, cols], y[:, cols])
